import numpy as np
import ml_dtypes


def mxq(x, axis, fmt="e4m3"):
    dtype, down = {"e4m3": (ml_dtypes.float8_e4m3fn, 7), "e5m2": (ml_dtypes.float8_e5m2, 14)}[fmt]
    v = np.moveaxis(np.asarray(x, np.float32).astype(ml_dtypes.bfloat16).astype(np.float64), axis, -1)
    blocks = v.reshape(v.shape[:-1] + (-1, 32))
    amax = np.abs(blocks).max(-1, keepdims=True)
    byte = np.maximum(np.where(amax > 0, np.frexp(amax)[1] - 1 + 127, 0) - down, 1)
    scale = np.exp2(byte - 127.0)
    codes = (blocks / scale).astype(np.float32).astype(dtype).astype(np.float64)
    return np.moveaxis((codes * scale).reshape(v.shape), -1, axis)


WIDE = False


def mx_kscale(k):
    if not WIDE:
        return np.ones(k)
    levels = np.array([30, -30])
    if k % 512:
        return np.exp2(np.random.permutation(np.resize(levels, k // 32))).repeat(32)
    a = np.empty((k // 512, 16))
    for p in range(k // 512):
        a[p, :8] = np.random.permutation(np.resize(levels, 8))
        for g in range(8):
            far = levels[np.abs(levels - a[p, g]) >= 10]
            a[p, g + 8] = far[np.random.randint(len(far))]
    return np.exp2(a.ravel()).repeat(32)


def f64(x):
    return np.asarray(x).astype(np.float64)


def striped8(idx):
    return np.asarray(idx).reshape(8, -1, 16).transpose(0, 2, 1).reshape(128, -1).astype(np.uint16)


def unstriped8(offs):
    return offs.reshape(8, 16, -1).transpose(0, 2, 1).reshape(8, -1).astype(np.int64)


def pick8(x, idx, run):
    r = np.arange(len(x))
    return x[r[:, None], idx[r % (8 * run) // run]]


E2M1 = np.array([0.0, 0.5, 1.0, 1.5, 2.0, 3.0, 4.0, 6.0, -0.0, -0.5, -1.0, -1.5, -2.0, -3.0, -4.0, -6.0])


def pack_weight(w, fmt):
    k, n = w.shape
    w = f64(np.asarray(w, np.float32).astype(ml_dtypes.bfloat16)).reshape(k // 32, 32, n)
    amax = np.abs(w).max(1)
    if fmt in ("e4m3", "e5m2"):
        byte = np.frexp(amax)[1] - 1 + 127 - (7 if fmt == "e4m3" else 14)
    else:
        mant, ex = np.frexp(amax / 6.0)
        byte = np.where(mant > 0.5, ex, ex - 1) + 127
    byte = np.clip(np.where(amax > 0, byte, 1), 1, 254)
    scaled = (w * np.exp2(127.0 - byte)[:, None, :]).reshape(k, n).astype(np.float32)
    by_word = np.ascontiguousarray(scaled.reshape(k // 512, 128, 4, n).transpose(0, 1, 3, 2))
    if fmt in ("e4m3", "e5m2"):
        words = by_word.astype(ml_dtypes.float8_e4m3fn if fmt == "e4m3" else ml_dtypes.float8_e5m2).view(np.uint8)
    else:
        c = by_word.astype(ml_dtypes.float4_e2m1fn).view(np.uint8) & 0xF
        words = (c[..., 0::2] | (c[..., 1::2] << 4)).reshape(k // 512, 128, 2 * n)
    return np.ascontiguousarray(words), np.ascontiguousarray(byte.astype(np.uint8).reshape(k // 512, 16, n))


def unpack_weight(words, scales, fmt):
    g, _, n = scales.shape
    words = np.ascontiguousarray(words).reshape(g, 128, n, -1)
    if fmt in ("e4m3", "e5m2"):
        vals = words.view(ml_dtypes.float8_e4m3fn if fmt == "e4m3" else ml_dtypes.float8_e5m2).astype(np.float64)
    else:
        nib = np.empty((g, 128, n, 4), np.uint8)
        nib[..., 0::2] = words & 0xF
        nib[..., 1::2] = words >> 4
        vals = E2M1[nib]
    vals = vals * np.repeat(np.exp2(scales.astype(np.float64) - 127.0), 8, axis=1)[..., None]
    return vals.transpose(0, 1, 3, 2).reshape(g * 512, n)


K, T, J, R, N = 1024, 512, 128, 512, 256


def setup_inputs():
    n = np.random.standard_normal
    idx = np.stack([np.random.permutation(T)[:J] for _ in range(8)])
    fk = mx_kscale(K)
    fr = mx_kscale(R)
    xtp = pack_weight(n((K, T)) / fk[:, None], "e5m2")
    wp = pack_weight(n((K, R)) * 1 / np.sqrt(K) * fk[:, None] * fr, "e4m3")
    wbp = pack_weight(n((R, N)) * 1 / np.sqrt(R) / fr[:, None], "e2m1")
    return {
        "xt_words": xtp[0],
        "xt_scales": xtp[1],
        "w_words": wp[0],
        "w_scales": wp[1],
        "wb_words": wbp[0],
        "wb_scales": wbp[1],
        "bi": (np.random.uniform(-0.5, 0.5, (1, N))).astype(np.float32),
        "offs": striped8(idx),
    }


def reference(xt_words, xt_scales, w_words, w_scales, wb_words, wb_scales, bi, offs):
    idx = unstriped8(offs)
    xtu = unpack_weight(xt_words, xt_scales, "e5m2")
    wu = unpack_weight(w_words, w_scales, "e4m3")
    wbu = unpack_weight(wb_words, wb_scales, "e2m1")
    xtidxg = pick8(xtu, idx, 64)
    a = wu.T @ xtidxg
    pk1 = np.max(a, axis=1, keepdims=True)
    hid = np.maximum(a - 0.4 * pk1, 0.0)
    hidq = mxq(hid, 0, "e5m2")
    p = hidq.T @ wbu
    ea = np.exp(0.7 * p + f64(bi))
    y = 256.0 * ea / np.sum(ea, axis=1, keepdims=True)
    return y

@@ -1,0 +1,157 @@
+from contextlib import ExitStack
+
+import concourse.mybir as mybir
+from concourse.masks import make_identity
+
+K, T, J, R, N = 1024, 512, 128, 512, 256
+FLOPS = 2 * K * R * J + 2 * R * J * N
+
+F32 = mybir.dt.float32
+BF16 = mybir.dt.bfloat16
+I32 = mybir.dt.int32
+U32 = mybir.dt.uint32
+U16 = mybir.dt.uint16
+U8 = mybir.dt.uint8
+E4M3X4 = mybir.dt.float8_e4m3fn_x4
+E5M2X4 = mybir.dt.float8_e5m2_x4
+E2M1X4 = mybir.dt.float4_e2m1fn_x4
+ALU = mybir.AluOpType
+ACT = mybir.ActivationFunctionType
+
+P = 128
+PACK = 4
+PASSES = K // (P * PACK)
+QUADS = 4
+
+
+def tile_list_headpicks_peakgated_rowshares_kernel(
+    tc, xt_words, xt_scales, w_words, w_scales, wb_words, wb_scales, bi, offs, out
+):
+    nc = tc.nc
+    with ExitStack() as ctx:
+        sb = ctx.enter_context(tc.tile_pool(name="sb", bufs=1))
+        ps = ctx.enter_context(tc.psum_pool(name="ps", bufs=1))
+
+        offsets = sb.tile([P, J // 16], U16, name="offsets")
+        nc.sync.dma_start(offsets[:], offs)
+
+        bi_col = sb.tile([P, 2], F32, name="bi_col")
+        nc.sync.dma_start(bi_col[:], bi.rearrange("o (p c) -> p (o c)", c=2))
+
+        xs = sb.tile([P, T], U8, name="xs", align_bytes=64)
+        nc.vector.memset(xs[:].bitcast(I32), 0)
+        nc.sync.dma_start(xs[0:P:4, :].bitcast(I32), xt_scales.bitcast(I32).rearrange("z q c -> q z c"))
+
+        ws_raw = sb.tile([P, PASSES * R], U8, name="ws_raw", align_bytes=64)
+        nc.vector.memset(ws_raw[:].bitcast(I32), 0)
+        for x in range(QUADS):
+            nc.scalar.dma_start(
+                ws_raw[32 * x : 32 * x + 4, :].bitcast(I32).rearrange("q (z c) -> q z c", z=PASSES),
+                w_scales.bitcast(I32)[:, 4 * x : 4 * x + 4, :].rearrange("z q c -> q z c"),
+            )
+        xs_plane = sb.tile([P, PASSES * J], U8, name="xs_plane", align_bytes=64)
+        nc.vector.memset(xs_plane[:].bitcast(I32), 0)
+
+        ww_raw = sb.tile([P, PASSES, R], U32, name="ww_raw", tag="weights_as_loaded", align_bytes=64)
+        nc.sync.dma_start(
+            ww_raw[:].bitcast(I32),
+            w_words.rearrange("z p c t -> p z (c t)").bitcast(I32),
+        )
+        xw = []
+        for z in range(PASSES):
+            xw_z = sb.tile([P, T], U32, name=f"xw{z}", align_bytes=64)
+            nc.sync.dma_start(xw_z[:].bitcast(I32), xt_words[z].rearrange("p c t -> p (c t)").bitcast(I32))
+            xw.append(xw_z)
+
+        ident = sb.tile([P, P], F32, name="ident", align_bytes=64)
+        make_identity(nc, ident[:])
+
+        xs_picked = sb.tile([P, J], U8, name="xs_picked", align_bytes=64)
+        nc.vector.tensor_copy(xs_picked[:], xs[:].indirect(offsets[:]))
+        for x in range(QUADS):
+            nc.sync.dma_start(
+                xs_plane[32 * x : 32 * x + 4, :].bitcast(I32).rearrange("q (z c) -> q z c", z=PASSES),
+                xs_picked[32 * x : 32 * x + 32 : 4, :].bitcast(I32),
+            )
+
+        ws = sb.tile([P, PASSES, PACK, P], U8, name="ws", align_bytes=64)
+        nc.vector.tensor_copy(
+            ws[:].rearrange("p z t (b m) -> p z b t m", m=16),
+            ws_raw[:].rearrange("p (z b m t) -> p z b t m", z=PASSES, m=16, t=PACK),
+        )
+        for x in range(QUADS):
+            nc.sync.dma_start(
+                ws_raw[32 * x : 32 * x + 4, 0:N].bitcast(I32),
+                wb_scales.bitcast(I32)[0, 4 * x : 4 * x + 4, :],
+            )
+        ww = sb.tile([P, PASSES, PACK, P], U32, name="ww", align_bytes=64)
+        nc.vector.tensor_copy(
+            ww[:].rearrange("p z t (b m) -> p z b t m", m=4),
+            ww_raw[:].rearrange("p z (b m t) -> p z b t m", m=4, t=PACK),
+        )
+        wbw = sb.tile([P, 2 * N], U8, name="wbw", tag="weights_as_loaded", align_bytes=64)
+        nc.sync.dma_start(wbw[:].bitcast(I32), wb_words[0].bitcast(I32))
+        xg = []
+        for z in range(PASSES):
+            xg_z = sb.tile([P, J], U32, name=f"xg{z}", align_bytes=64)
+            nc.vector.tensor_copy(xg_z[:], xw[z][:].indirect(offsets[:]))
+            xg.append(xg_z)
+
+        hid_rows = sb.tile([P, PACK, J], BF16, name="hid_rows", align_bytes=64)
+        for t in range(PACK):
+            a_t = ps.tile([P, J], F32, name=f"a{t}", tag=f"a{t}")
+            for z in range(PASSES):
+                nc.tensor.matmul_mx(
+                    a_t[:],
+                    lhsT=ww[:, z, t, :].bitcast(E4M3X4),
+                    lhsT_scale=ws[:, z, t, :],
+                    rhs=xg[z][:].bitcast(E5M2X4),
+                    rhs_scale=xs_plane[:, z * J : (z + 1) * J],
+                    start=(z == 0),
+                    stop=(z == PASSES - 1),
+                )
+            scaled = sb.tile([P, J], F32, name=f"scaled{t}", align_bytes=64)
+            floor = sb.tile([P, 1], F32, name=f"floor{t}")
+            nc.vector.tensor_scalar(scaled[:], a_t[:], -0.4, None, ALU.mult, ALU.min, accum_out=floor[:])
+            nc.scalar.activation(hid_rows[:, t, :], scaled[:], ACT.Relu, bias=floor[:], scale=-2.5)
+
+        bias_ps = ps.tile([P, 2, P], F32, name="bias_ps", tag=f"a{PACK - 1}")
+        for c in range(2):
+            nc.tensor.transpose(bias_ps[:, c, :], bi_col[:, c : c + 1].to_broadcast([P, P]), ident[:])
+        bias = sb.tile([P, P, 2], F32, name="bias", align_bytes=64)
+        nc.scalar.activation(bias[:], bias_ps[:].rearrange("j c p -> j p c"), ACT.Copy)
+
+        hid = sb.tile([P, J, PACK], BF16, name="hid", align_bytes=64)
+        nc.vector.tensor_copy(
+            hid[:].rearrange("p (c i) t -> p c t i", i=4),
+            hid_rows[:].rearrange("p t (c i) -> p c t i", i=4),
+        )
+        hq = sb.tile([P, J], U32, name="hq", align_bytes=64)
+        hs = sb.tile([P, J], U8, name="hs", align_bytes=64)
+        nc.vector.quantize_mx(hq[:].bitcast(E5M2X4), hs[:], hid[:].rearrange("p j t -> p (j t)"))
+
+        p_ps = ps.tile([J, N], F32, name="p_ps")
+        nc.tensor.matmul_mx(
+            p_ps[:],
+            lhsT=hq[:].bitcast(E5M2X4),
+            lhsT_scale=hs[:],
+            rhs=wbw[:].bitcast(E2M1X4),
+            rhs_scale=ws_raw[:, 0:N],
+            start=True,
+            stop=True,
+        )
+
+        neg_z = sb.tile([J, N], F32, name="neg_z", align_bytes=64)
+        nc.vector.scalar_tensor_tensor(
+            neg_z[:], p_ps[:], -0.7, bias[:].rearrange("j p c -> j (p c)"), ALU.mult, ALU.subtract
+        )
+        neg_peak = sb.tile([J, 1], F32, name="neg_peak")
+        nc.vector.tensor_reduce(neg_peak[:], neg_z[:], mybir.AxisListType.X, ALU.min)
+        ea = sb.tile([J, N], F32, name="ea", align_bytes=64)
+        total = sb.tile([J, 1], F32, name="total")
+        nc.scalar.activation(ea[:], neg_z[:], ACT.Exp, bias=neg_peak[:], scale=-1.0, accum_out=total[:])
+        inv = sb.tile([J, 1], F32, name="inv")
+        nc.vector.reciprocal(inv[:], total[:])
+        y = sb.tile([J, N], F32, name="y", align_bytes=64)
+        nc.vector.tensor_scalar(y[:], ea[:], inv[:], 256.0, ALU.mult, ALU.mult)
+        nc.sync.dma_start(out, y[:])

@@ -22,6 +22,10 @@ P = 128
 PACK = 4
 PASSES = K // (P * PACK)
 QUADS = 4
+HALF = N // 2
+X_AT = R
+WB_AT = X_AT + J
+ROW = WB_AT + HALF
 
 
 def tile_list_headpicks_peakgated_rowshares_kernel(
@@ -35,22 +39,23 @@ def tile_list_headpicks_peakgated_rowshares_kernel(
         offsets = sb.tile([P, J // 16], U16, name="offsets")
         nc.sync.dma_start(offsets[:], offs)
 
-        bi_col = sb.tile([P, 2], F32, name="bi_col")
-        nc.sync.dma_start(bi_col[:], bi.rearrange("o (p c) -> p (o c)", c=2))
-
+        staged = sb.tile([P, ROW], U8, name="staged", align_bytes=64)
+        nc.sync.dma_start(
+            staged[0:P:4, WB_AT:ROW].bitcast(I32),
+            wb_scales.bitcast(I32)[0].rearrange("q (h c) -> (q h) c", h=2),
+        )
         xs = sb.tile([P, T], U8, name="xs", align_bytes=64)
         nc.vector.memset(xs[:].bitcast(I32), 0)
         nc.sync.dma_start(xs[0:P:4, :].bitcast(I32), xt_scales.bitcast(I32).rearrange("z q c -> q z c"))
 
-        ws_raw = sb.tile([P, PASSES * R], U8, name="ws_raw", align_bytes=64)
-        nc.vector.memset(ws_raw[:].bitcast(I32), 0)
-        for x in range(QUADS):
-            nc.scalar.dma_start(
-                ws_raw[32 * x : 32 * x + 4, :].bitcast(I32).rearrange("q (z c) -> q z c", z=PASSES),
-                w_scales.bitcast(I32)[:, 4 * x : 4 * x + 4, :].rearrange("z q c -> q z c"),
-            )
-        xs_plane = sb.tile([P, PASSES * J], U8, name="xs_plane", align_bytes=64)
-        nc.vector.memset(xs_plane[:].bitcast(I32), 0)
+        bi_col = sb.tile([P, 2], F32, name="bi_col")
+        nc.scalar.dma_start(bi_col[:], bi.rearrange("o (p c) -> p (o c)", c=2))
+        ws_raw = sb.tile([P, R], U8, name="ws_raw", align_bytes=64)
+        nc.gpsimd.memset(ws_raw[:].bitcast(I32), 0)
+        nc.sync.dma_start(ws_raw[0:P:4, :].bitcast(I32), w_scales.bitcast(I32).rearrange("z q c -> q z c"))
+
+        planes = sb.tile([P, 2, ROW], U8, name="planes", align_bytes=64)
+        nc.vector.memset(planes[:].bitcast(I32), 0)
 
         ww_raw = sb.tile([P, PASSES, R], U32, name="ww_raw", tag="weights_as_loaded", align_bytes=64)
         nc.sync.dma_start(
@@ -68,22 +73,18 @@ def tile_list_headpicks_peakgated_rowshares_kernel(
 
         xs_picked = sb.tile([P, J], U8, name="xs_picked", align_bytes=64)
         nc.vector.tensor_copy(xs_picked[:], xs[:].indirect(offsets[:]))
+        nc.vector.tensor_copy(
+            staged[:, 0:X_AT].rearrange("p (t b m) -> p b t m", t=PACK, m=16),
+            ws_raw[:].rearrange("p (b m t) -> p b t m", m=16, t=PACK),
+        )
+        nc.vector.tensor_copy(staged[:, X_AT:WB_AT].bitcast(I32), xs_picked[:].bitcast(I32))
         for x in range(QUADS):
-            nc.sync.dma_start(
-                xs_plane[32 * x : 32 * x + 4, :].bitcast(I32).rearrange("q (z c) -> q z c", z=PASSES),
-                xs_picked[32 * x : 32 * x + 32 : 4, :].bitcast(I32),
+            queue = nc.sync if x % 2 == 0 else nc.scalar
+            queue.dma_start(
+                planes[32 * x : 32 * x + 4, :, :].bitcast(I32),
+                staged[32 * x : 32 * x + 32 : 4, :].bitcast(I32),
             )
 
-        ws = sb.tile([P, PASSES, PACK, P], U8, name="ws", align_bytes=64)
-        nc.vector.tensor_copy(
-            ws[:].rearrange("p z t (b m) -> p z b t m", m=16),
-            ws_raw[:].rearrange("p (z b m t) -> p z b t m", z=PASSES, m=16, t=PACK),
-        )
-        for x in range(QUADS):
-            nc.sync.dma_start(
-                ws_raw[32 * x : 32 * x + 4, 0:N].bitcast(I32),
-                wb_scales.bitcast(I32)[0, 4 * x : 4 * x + 4, :],
-            )
         ww = sb.tile([P, PASSES, PACK, P], U32, name="ww", align_bytes=64)
         nc.vector.tensor_copy(
             ww[:].rearrange("p z t (b m) -> p z b t m", m=4),
@@ -104,9 +105,9 @@ def tile_list_headpicks_peakgated_rowshares_kernel(
                 nc.tensor.matmul_mx(
                     a_t[:],
                     lhsT=ww[:, z, t, :].bitcast(E4M3X4),
-                    lhsT_scale=ws[:, z, t, :],
+                    lhsT_scale=planes[:, z, t * P : (t + 1) * P],
                     rhs=xg[z][:].bitcast(E5M2X4),
-                    rhs_scale=xs_plane[:, z * J : (z + 1) * J],
+                    rhs_scale=planes[:, z, X_AT:WB_AT],
                     start=(z == 0),
                     stop=(z == PASSES - 1),
                 )
@@ -130,21 +131,21 @@ def tile_list_headpicks_peakgated_rowshares_kernel(
         hs = sb.tile([P, J], U8, name="hs", align_bytes=64)
         nc.vector.quantize_mx(hq[:].bitcast(E5M2X4), hs[:], hid[:].rearrange("p j t -> p (j t)"))
 
-        p_ps = ps.tile([J, N], F32, name="p_ps")
-        nc.tensor.matmul_mx(
-            p_ps[:],
-            lhsT=hq[:].bitcast(E5M2X4),
-            lhsT_scale=hs[:],
-            rhs=wbw[:].bitcast(E2M1X4),
-            rhs_scale=ws_raw[:, 0:N],
-            start=True,
-            stop=True,
-        )
-
         neg_z = sb.tile([J, N], F32, name="neg_z", align_bytes=64)
-        nc.vector.scalar_tensor_tensor(
-            neg_z[:], p_ps[:], -0.7, bias[:].rearrange("j p c -> j (p c)"), ALU.mult, ALU.subtract
-        )
+        bias_row = bias[:].rearrange("j p c -> j (p c)")
+        for h in range(2):
+            cols = slice(h * HALF, (h + 1) * HALF)
+            p_h = ps.tile([J, HALF], F32, name=f"p{h}")
+            nc.tensor.matmul_mx(
+                p_h[:],
+                lhsT=hq[:].bitcast(E5M2X4),
+                lhsT_scale=hs[:],
+                rhs=wbw[:, 2 * h * HALF : 2 * (h + 1) * HALF].bitcast(E2M1X4),
+                rhs_scale=planes[:, h, WB_AT:ROW],
+                start=True,
+                stop=True,
+            )
+            nc.vector.scalar_tensor_tensor(neg_z[:, cols], p_h[:], -0.7, bias_row[:, cols], ALU.mult, ALU.subtract)
         neg_peak = sb.tile([J, 1], F32, name="neg_peak")
         nc.vector.tensor_reduce(neg_peak[:], neg_z[:], mybir.AxisListType.X, ALU.min)
         ea = sb.tile([J, N], F32, name="ea", align_bytes=64)

@@ -39,20 +39,20 @@ def tile_list_headpicks_peakgated_rowshares_kernel(
         offsets = sb.tile([P, J // 16], U16, name="offsets")
         nc.sync.dma_start(offsets[:], offs)
 
-        staged = sb.tile([P, ROW], U8, name="staged", align_bytes=64)
-        nc.sync.dma_start(
-            staged[0:P:4, WB_AT:ROW].bitcast(I32),
-            wb_scales.bitcast(I32)[0].rearrange("q (h c) -> (q h) c", h=2),
-        )
         xs = sb.tile([P, T], U8, name="xs", align_bytes=64)
         nc.vector.memset(xs[:].bitcast(I32), 0)
         nc.sync.dma_start(xs[0:P:4, :].bitcast(I32), xt_scales.bitcast(I32).rearrange("z q c -> q z c"))
 
-        bi_col = sb.tile([P, 2], F32, name="bi_col")
-        nc.scalar.dma_start(bi_col[:], bi.rearrange("o (p c) -> p (o c)", c=2))
+        staged = sb.tile([P, ROW], U8, name="staged", align_bytes=64)
+        nc.scalar.dma_start(
+            staged[0:P:4, WB_AT:ROW].bitcast(I32),
+            wb_scales.bitcast(I32)[0].rearrange("q (h c) -> (q h) c", h=2),
+        )
         ws_raw = sb.tile([P, R], U8, name="ws_raw", align_bytes=64)
         nc.gpsimd.memset(ws_raw[:].bitcast(I32), 0)
-        nc.sync.dma_start(ws_raw[0:P:4, :].bitcast(I32), w_scales.bitcast(I32).rearrange("z q c -> q z c"))
+        nc.scalar.dma_start(ws_raw[0:P:4, :].bitcast(I32), w_scales.bitcast(I32).rearrange("z q c -> q z c"))
+        bi_col = sb.tile([P, 2], F32, name="bi_col")
+        nc.scalar.dma_start(bi_col[:], bi.rearrange("o (p c) -> p (o c)", c=2))
 
         planes = sb.tile([P, 2, ROW], U8, name="planes", align_bytes=64)
         nc.vector.memset(planes[:].bitcast(I32), 0)
@@ -98,7 +98,7 @@ def tile_list_headpicks_peakgated_rowshares_kernel(
             nc.vector.tensor_copy(xg_z[:], xw[z][:].indirect(offsets[:]))
             xg.append(xg_z)
 
-        hid_rows = sb.tile([P, PACK, J], BF16, name="hid_rows", align_bytes=64)
+        hid_pairs = sb.tile([P, 2, J, 2], BF16, name="hid_pairs", align_bytes=64)
         for t in range(PACK):
             a_t = ps.tile([P, J], F32, name=f"a{t}", tag=f"a{t}")
             for z in range(PASSES):
@@ -114,7 +114,7 @@ def tile_list_headpicks_peakgated_rowshares_kernel(
             scaled = sb.tile([P, J], F32, name=f"scaled{t}", align_bytes=64)
             floor = sb.tile([P, 1], F32, name=f"floor{t}")
             nc.vector.tensor_scalar(scaled[:], a_t[:], -0.4, None, ALU.mult, ALU.min, accum_out=floor[:])
-            nc.scalar.activation(hid_rows[:, t, :], scaled[:], ACT.Relu, bias=floor[:], scale=-2.5)
+            nc.scalar.activation(hid_pairs[:, t // 2, :, t % 2], scaled[:], ACT.Relu, bias=floor[:], scale=-2.5)
 
         bias_ps = ps.tile([P, 2, P], F32, name="bias_ps", tag=f"a{PACK - 1}")
         for c in range(2):
@@ -124,8 +124,8 @@ def tile_list_headpicks_peakgated_rowshares_kernel(
 
         hid = sb.tile([P, J, PACK], BF16, name="hid", align_bytes=64)
         nc.vector.tensor_copy(
-            hid[:].rearrange("p (c i) t -> p c t i", i=4),
-            hid_rows[:].rearrange("p t (c i) -> p c t i", i=4),
+            hid[:].bitcast(F32),
+            hid_pairs[:].rearrange("p u j e -> p u (j e)").bitcast(F32).rearrange("p u j -> p j u"),
         )
         hq = sb.tile([P, J], U32, name="hq", align_bytes=64)
         hs = sb.tile([P, J], U8, name="hs", align_bytes=64)

@@ -23,9 +23,6 @@ PACK = 4
 PASSES = K // (P * PACK)
 QUADS = 4
 HALF = N // 2
-X_AT = R
-WB_AT = X_AT + J
-ROW = WB_AT + HALF
 
 
 def tile_list_headpicks_peakgated_rowshares_kernel(
@@ -39,23 +36,24 @@ def tile_list_headpicks_peakgated_rowshares_kernel(
         offsets = sb.tile([P, J // 16], U16, name="offsets")
         nc.sync.dma_start(offsets[:], offs)
 
-        xs = sb.tile([P, T], U8, name="xs", align_bytes=64)
+        xs = sb.tile([P, T], U8, name="xs", tag="xs", align_bytes=64)
         nc.vector.memset(xs[:].bitcast(I32), 0)
         nc.sync.dma_start(xs[0:P:4, :].bitcast(I32), xt_scales.bitcast(I32).rearrange("z q c -> q z c"))
 
-        staged = sb.tile([P, ROW], U8, name="staged", align_bytes=64)
-        nc.scalar.dma_start(
-            staged[0:P:4, WB_AT:ROW].bitcast(I32),
-            wb_scales.bitcast(I32)[0].rearrange("q (h c) -> (q h) c", h=2),
-        )
-        ws_raw = sb.tile([P, R], U8, name="ws_raw", align_bytes=64)
-        nc.gpsimd.memset(ws_raw[:].bitcast(I32), 0)
-        nc.scalar.dma_start(ws_raw[0:P:4, :].bitcast(I32), w_scales.bitcast(I32).rearrange("z q c -> q z c"))
-        bi_col = sb.tile([P, 2], F32, name="bi_col")
-        nc.scalar.dma_start(bi_col[:], bi.rearrange("o (p c) -> p (o c)", c=2))
+        ws_raw = sb.tile([P, PASSES * R], U8, name="ws_raw", align_bytes=64)
+        nc.vector.memset(ws_raw[:].bitcast(I32), 0)
+        for x in range(QUADS):
+            queue = nc.scalar if x < 2 else nc.sync
+            queue.dma_start(
+                ws_raw[32 * x : 32 * x + 4, :].bitcast(I32).rearrange("q (z c) -> q z c", z=PASSES),
+                w_scales.bitcast(I32)[:, 4 * x : 4 * x + 4, :].rearrange("z q c -> q z c"),
+            )
+        xs_plane = sb.tile([P, PASSES * J], U8, name="xs_plane", align_bytes=64)
+        nc.vector.memset(xs_plane[:].bitcast(I32), 0)
 
-        planes = sb.tile([P, 2, ROW], U8, name="planes", align_bytes=64)
-        nc.vector.memset(planes[:].bitcast(I32), 0)
+        ident = sb.tile([P, P], F32, name="ident", align_bytes=64)
+        nc.vector.memset(ident[:], 0.0)
+        make_identity(nc, ident[:], nomemset=True)
 
         ww_raw = sb.tile([P, PASSES, R], U32, name="ww_raw", tag="weights_as_loaded", align_bytes=64)
         nc.sync.dma_start(
@@ -68,23 +66,29 @@ def tile_list_headpicks_peakgated_rowshares_kernel(
             nc.sync.dma_start(xw_z[:].bitcast(I32), xt_words[z].rearrange("p c t -> p (c t)").bitcast(I32))
             xw.append(xw_z)
 
-        ident = sb.tile([P, P], F32, name="ident", align_bytes=64)
-        make_identity(nc, ident[:])
 
         xs_picked = sb.tile([P, J], U8, name="xs_picked", align_bytes=64)
         nc.vector.tensor_copy(xs_picked[:], xs[:].indirect(offsets[:]))
-        nc.vector.tensor_copy(
-            staged[:, 0:X_AT].rearrange("p (t b m) -> p b t m", t=PACK, m=16),
-            ws_raw[:].rearrange("p (b m t) -> p b t m", m=16, t=PACK),
-        )
-        nc.vector.tensor_copy(staged[:, X_AT:WB_AT].bitcast(I32), xs_picked[:].bitcast(I32))
         for x in range(QUADS):
             queue = nc.sync if x % 2 == 0 else nc.scalar
             queue.dma_start(
-                planes[32 * x : 32 * x + 4, :, :].bitcast(I32),
-                staged[32 * x : 32 * x + 32 : 4, :].bitcast(I32),
+                xs_plane[32 * x : 32 * x + 4, :].bitcast(I32).rearrange("q (z c) -> q z c", z=PASSES),
+                xs_picked[32 * x : 32 * x + 32 : 4, :].bitcast(I32),
             )
 
+        bi_col = sb.tile([P, 2], F32, name="bi_col", tag="xs", align_bytes=64)
+        nc.scalar.dma_start(bi_col[:], bi.rearrange("o (p c) -> p (o c)", c=2))
+
+        ws = sb.tile([P, PASSES, PACK, P], U8, name="ws", align_bytes=64)
+        nc.vector.tensor_copy(
+            ws[:].rearrange("p z t (b m) -> p z b t m", m=16),
+            ws_raw[:].rearrange("p (z b m t) -> p z b t m", z=PASSES, m=16, t=PACK),
+        )
+        for x in range(QUADS):
+            nc.sync.dma_start(
+                ws_raw[32 * x : 32 * x + 4, 0:N].bitcast(I32),
+                wb_scales.bitcast(I32)[0, 4 * x : 4 * x + 4, :],
+            )
         ww = sb.tile([P, PASSES, PACK, P], U32, name="ww", align_bytes=64)
         nc.vector.tensor_copy(
             ww[:].rearrange("p z t (b m) -> p z b t m", m=4),
@@ -105,9 +109,9 @@ def tile_list_headpicks_peakgated_rowshares_kernel(
                 nc.tensor.matmul_mx(
                     a_t[:],
                     lhsT=ww[:, z, t, :].bitcast(E4M3X4),
-                    lhsT_scale=planes[:, z, t * P : (t + 1) * P],
+                    lhsT_scale=ws[:, z, t, :],
                     rhs=xg[z][:].bitcast(E5M2X4),
-                    rhs_scale=planes[:, z, X_AT:WB_AT],
+                    rhs_scale=xs_plane[:, z * J : (z + 1) * J],
                     start=(z == 0),
                     stop=(z == PASSES - 1),
                 )
@@ -141,7 +145,7 @@ def tile_list_headpicks_peakgated_rowshares_kernel(
                 lhsT=hq[:].bitcast(E5M2X4),
                 lhsT_scale=hs[:],
                 rhs=wbw[:, 2 * h * HALF : 2 * (h + 1) * HALF].bitcast(E2M1X4),
-                rhs_scale=planes[:, h, WB_AT:ROW],
+                rhs_scale=ws_raw[:, cols],
                 start=True,
                 stop=True,
             )

@@ -102,7 +102,8 @@ def tile_list_headpicks_peakgated_rowshares_kernel(
             nc.vector.tensor_copy(xg_z[:], xw[z][:].indirect(offsets[:]))
             xg.append(xg_z)
 
-        hid_pairs = sb.tile([P, 2, J, 2], BF16, name="hid_pairs", align_bytes=64)
+        first_pair = sb.tile([P, J, 2], BF16, name="first_pair", align_bytes=64)
+        hid = sb.tile([P, J, PACK], BF16, name="hid", align_bytes=64)
         for t in range(PACK):
             a_t = ps.tile([P, J], F32, name=f"a{t}", tag=f"a{t}")
             for z in range(PASSES):
@@ -118,7 +119,8 @@ def tile_list_headpicks_peakgated_rowshares_kernel(
             scaled = sb.tile([P, J], F32, name=f"scaled{t}", align_bytes=64)
             floor = sb.tile([P, 1], F32, name=f"floor{t}")
             nc.vector.tensor_scalar(scaled[:], a_t[:], -0.4, None, ALU.mult, ALU.min, accum_out=floor[:])
-            nc.scalar.activation(hid_pairs[:, t // 2, :, t % 2], scaled[:], ACT.Relu, bias=floor[:], scale=-2.5)
+            rows = first_pair[:, :, t] if t < 2 else hid[:, :, t]
+            nc.scalar.activation(rows, scaled[:], ACT.Relu, bias=floor[:], scale=-2.5)
 
         bias_ps = ps.tile([P, 2, P], F32, name="bias_ps", tag=f"a{PACK - 1}")
         for c in range(2):
@@ -126,11 +128,7 @@ def tile_list_headpicks_peakgated_rowshares_kernel(
         bias = sb.tile([P, P, 2], F32, name="bias", align_bytes=64)
         nc.scalar.activation(bias[:], bias_ps[:].rearrange("j c p -> j p c"), ACT.Copy)
 
-        hid = sb.tile([P, J, PACK], BF16, name="hid", align_bytes=64)
-        nc.vector.tensor_copy(
-            hid[:].bitcast(F32),
-            hid_pairs[:].rearrange("p u j e -> p u (j e)").bitcast(F32).rearrange("p u j -> p j u"),
-        )
+        nc.vector.tensor_copy(hid[:, :, 0:2], first_pair[:])
         hq = sb.tile([P, J], U32, name="hq", align_bytes=64)
         hs = sb.tile([P, J], U8, name="hs", align_bytes=64)
         nc.vector.quantize_mx(hq[:].bitcast(E5M2X4), hs[:], hid[:].rearrange("p j t -> p (j t)"))

from contextlib import ExitStack

import concourse.mybir as mybir
from concourse.masks import make_identity

K, T, J, R, N = 1024, 512, 128, 512, 256
FLOPS = 2 * K * R * J + 2 * R * J * N

F32 = mybir.dt.float32
BF16 = mybir.dt.bfloat16
I32 = mybir.dt.int32
U32 = mybir.dt.uint32
U16 = mybir.dt.uint16
U8 = mybir.dt.uint8
E4M3X4 = mybir.dt.float8_e4m3fn_x4
E5M2X4 = mybir.dt.float8_e5m2_x4
E2M1X4 = mybir.dt.float4_e2m1fn_x4
ALU = mybir.AluOpType
ACT = mybir.ActivationFunctionType

P = 128
PACK = 4
PASSES = K // (P * PACK)
QUADS = 4
HALF = N // 2


def tile_list_headpicks_peakgated_rowshares_kernel(
    tc, xt_words, xt_scales, w_words, w_scales, wb_words, wb_scales, bi, offs, out
):
    nc = tc.nc
    with ExitStack() as ctx:
        sb = ctx.enter_context(tc.tile_pool(name="sb", bufs=1))
        ps = ctx.enter_context(tc.psum_pool(name="ps", bufs=1))

        offsets = sb.tile([P, J // 16], U16, name="offsets")
        nc.sync.dma_start(offsets[:], offs)

        xs = sb.tile([P, T], U8, name="xs", tag="xs", align_bytes=64)
        nc.vector.memset(xs[:].bitcast(I32), 0)
        nc.sync.dma_start(xs[0:P:4, :].bitcast(I32), xt_scales.bitcast(I32).rearrange("z q c -> q z c"))

        ws_raw = sb.tile([P, PASSES * R], U8, name="ws_raw", align_bytes=64)
        nc.vector.memset(ws_raw[:].bitcast(I32), 0)
        for x in range(QUADS):
            queue = nc.scalar if x < 2 else nc.sync
            queue.dma_start(
                ws_raw[32 * x : 32 * x + 4, :].bitcast(I32).rearrange("q (z c) -> q z c", z=PASSES),
                w_scales.bitcast(I32)[:, 4 * x : 4 * x + 4, :].rearrange("z q c -> q z c"),
            )
        xs_plane = sb.tile([P, PASSES * J], U8, name="xs_plane", align_bytes=64)
        nc.vector.memset(xs_plane[:].bitcast(I32), 0)

        ident = sb.tile([P, P], F32, name="ident", align_bytes=64)
        nc.vector.memset(ident[:], 0.0)
        make_identity(nc, ident[:], nomemset=True)

        ww_raw = sb.tile([P, PASSES, R], U32, name="ww_raw", tag="weights_as_loaded", align_bytes=64)
        nc.sync.dma_start(
            ww_raw[:].bitcast(I32),
            w_words.rearrange("z p c t -> p z (c t)").bitcast(I32),
        )
        xw = []
        for z in range(PASSES):
            xw_z = sb.tile([P, T], U32, name=f"xw{z}", align_bytes=64)
            nc.sync.dma_start(xw_z[:].bitcast(I32), xt_words[z].rearrange("p c t -> p (c t)").bitcast(I32))
            xw.append(xw_z)


        xs_picked = sb.tile([P, J], U8, name="xs_picked", align_bytes=64)
        nc.vector.tensor_copy(xs_picked[:], xs[:].indirect(offsets[:]))
        for x in range(QUADS):
            queue = nc.sync if x % 2 == 0 else nc.scalar
            queue.dma_start(
                xs_plane[32 * x : 32 * x + 4, :].bitcast(I32).rearrange("q (z c) -> q z c", z=PASSES),
                xs_picked[32 * x : 32 * x + 32 : 4, :].bitcast(I32),
            )

        bi_col = sb.tile([P, 2], F32, name="bi_col", tag="xs", align_bytes=64)
        nc.scalar.dma_start(bi_col[:], bi.rearrange("o (p c) -> p (o c)", c=2))

        ws = sb.tile([P, PASSES, PACK, P], U8, name="ws", align_bytes=64)
        nc.vector.tensor_copy(
            ws[:].rearrange("p z t (b m) -> p z b t m", m=16),
            ws_raw[:].rearrange("p (z b m t) -> p z b t m", z=PASSES, m=16, t=PACK),
        )
        for x in range(QUADS):
            nc.sync.dma_start(
                ws_raw[32 * x : 32 * x + 4, 0:N].bitcast(I32),
                wb_scales.bitcast(I32)[0, 4 * x : 4 * x + 4, :],
            )
        ww = sb.tile([P, PASSES, PACK, P], U32, name="ww", align_bytes=64)
        nc.vector.tensor_copy(
            ww[:].rearrange("p z t (b m) -> p z b t m", m=4),
            ww_raw[:].rearrange("p z (b m t) -> p z b t m", m=4, t=PACK),
        )
        wbw = sb.tile([P, 2 * N], U8, name="wbw", tag="weights_as_loaded", align_bytes=64)
        nc.sync.dma_start(wbw[:].bitcast(I32), wb_words[0].bitcast(I32))
        xg = []
        for z in range(PASSES):
            xg_z = sb.tile([P, J], U32, name=f"xg{z}", align_bytes=64)
            nc.vector.tensor_copy(xg_z[:], xw[z][:].indirect(offsets[:]))
            xg.append(xg_z)

        first_pair = sb.tile([P, J, 2], BF16, name="first_pair", align_bytes=64)
        hid = sb.tile([P, J, PACK], BF16, name="hid", align_bytes=64)
        for t in range(PACK):
            a_t = ps.tile([P, J], F32, name=f"a{t}", tag=f"a{t}")
            for z in range(PASSES):
                nc.tensor.matmul_mx(
                    a_t[:],
                    lhsT=ww[:, z, t, :].bitcast(E4M3X4),
                    lhsT_scale=ws[:, z, t, :],
                    rhs=xg[z][:].bitcast(E5M2X4),
                    rhs_scale=xs_plane[:, z * J : (z + 1) * J],
                    start=(z == 0),
                    stop=(z == PASSES - 1),
                )
            scaled = sb.tile([P, J], F32, name=f"scaled{t}", align_bytes=64)
            floor = sb.tile([P, 1], F32, name=f"floor{t}")
            nc.vector.tensor_scalar(scaled[:], a_t[:], -0.4, None, ALU.mult, ALU.min, accum_out=floor[:])
            rows = first_pair[:, :, t] if t < 2 else hid[:, :, t]
            nc.scalar.activation(rows, scaled[:], ACT.Relu, bias=floor[:], scale=-2.5)

        bias_ps = ps.tile([P, 2, P], F32, name="bias_ps", tag=f"a{PACK - 1}")
        for c in range(2):
            nc.tensor.transpose(bias_ps[:, c, :], bi_col[:, c : c + 1].to_broadcast([P, P]), ident[:])
        bias = sb.tile([P, P, 2], F32, name="bias", align_bytes=64)
        nc.scalar.activation(bias[:], bias_ps[:].rearrange("j c p -> j p c"), ACT.Copy)

        nc.vector.tensor_copy(hid[:, :, 0:2], first_pair[:])
        hq = sb.tile([P, J], U32, name="hq", align_bytes=64)
        hs = sb.tile([P, J], U8, name="hs", align_bytes=64)
        nc.vector.quantize_mx(hq[:].bitcast(E5M2X4), hs[:], hid[:].rearrange("p j t -> p (j t)"))

        neg_z = sb.tile([J, N], F32, name="neg_z", align_bytes=64)
        bias_row = bias[:].rearrange("j p c -> j (p c)")
        for h in range(2):
            cols = slice(h * HALF, (h + 1) * HALF)
            p_h = ps.tile([J, HALF], F32, name=f"p{h}")
            nc.tensor.matmul_mx(
                p_h[:],
                lhsT=hq[:].bitcast(E5M2X4),
                lhsT_scale=hs[:],
                rhs=wbw[:, 2 * h * HALF : 2 * (h + 1) * HALF].bitcast(E2M1X4),
                rhs_scale=ws_raw[:, cols],
                start=True,
                stop=True,
            )
            nc.vector.scalar_tensor_tensor(neg_z[:, cols], p_h[:], -0.7, bias_row[:, cols], ALU.mult, ALU.subtract)
        neg_peak = sb.tile([J, 1], F32, name="neg_peak")
        nc.vector.tensor_reduce(neg_peak[:], neg_z[:], mybir.AxisListType.X, ALU.min)
        ea = sb.tile([J, N], F32, name="ea", align_bytes=64)
        total = sb.tile([J, 1], F32, name="total")
        nc.scalar.activation(ea[:], neg_z[:], ACT.Exp, bias=neg_peak[:], scale=-1.0, accum_out=total[:])
        inv = sb.tile([J, 1], F32, name="inv")
        nc.vector.reciprocal(inv[:], total[:])
        y = sb.tile([J, N], F32, name="y", align_bytes=64)
        nc.vector.tensor_scalar(y[:], ea[:], inv[:], 256.0, ALU.mult, ALU.mult)
        nc.sync.dma_start(out, y[:])
